import numpy as np
import ml_dtypes


def mxq(x, axis, fmt="e4m3"):
    dtype, down = {"e4m3": (ml_dtypes.float8_e4m3fn, 7), "e5m2": (ml_dtypes.float8_e5m2, 14)}[fmt]
    v = np.moveaxis(np.asarray(x, np.float32).astype(ml_dtypes.bfloat16).astype(np.float64), axis, -1)
    blocks = v.reshape(v.shape[:-1] + (-1, 32))
    amax = np.abs(blocks).max(-1, keepdims=True)
    byte = np.maximum(np.where(amax > 0, np.frexp(amax)[1] - 1 + 127, 0) - down, 1)
    scale = np.exp2(byte - 127.0)
    codes = (blocks / scale).astype(np.float32).astype(dtype).astype(np.float64)
    return np.moveaxis((codes * scale).reshape(v.shape), -1, axis)


WIDE = False


def mx_kscale(k):
    if not WIDE:
        return np.ones(k)
    levels = np.array([10, -10, 5, -5, 0])
    if k % 512:
        return np.exp2(np.random.permutation(np.resize(levels, k // 32))).repeat(32)
    a = np.empty((k // 512, 16))
    for p in range(k // 512):
        a[p, :8] = np.random.permutation(np.resize(levels, 8))
        for g in range(8):
            far = levels[np.abs(levels - a[p, g]) >= 10]
            a[p, g + 8] = far[np.random.randint(len(far))]
    return np.exp2(a.ravel()).repeat(32)


def f64(x):
    return np.asarray(x).astype(np.float64)


def striped(idx):
    return np.tile(idx.reshape(-1, 16).T, (8, 1)).astype(np.uint16)


def unstriped(offs):
    return offs[:16].T.reshape(-1).astype(np.int64)


E2M1 = np.array([0.0, 0.5, 1.0, 1.5, 2.0, 3.0, 4.0, 6.0, -0.0, -0.5, -1.0, -1.5, -2.0, -3.0, -4.0, -6.0])


def pack_weight(w, fmt):
    k, n = w.shape
    w = f64(np.asarray(w, np.float32).astype(ml_dtypes.bfloat16)).reshape(k // 32, 32, n)
    amax = np.abs(w).max(1)
    if fmt == "e4m3":
        byte = np.frexp(amax)[1] - 1 + 127 - 7
    else:
        mant, ex = np.frexp(amax / 6.0)
        byte = np.where(mant > 0.5, ex, ex - 1) + 127
    byte = np.clip(np.where(amax > 0, byte, 1), 1, 254)
    scaled = (w * np.exp2(127.0 - byte)[:, None, :]).reshape(k, n).astype(np.float32)
    by_word = np.ascontiguousarray(scaled.reshape(k // 512, 128, 4, n).transpose(0, 1, 3, 2))
    if fmt == "e4m3":
        words = by_word.astype(ml_dtypes.float8_e4m3fn).view(np.uint8)
    else:
        c = by_word.astype(ml_dtypes.float4_e2m1fn).view(np.uint8) & 0xF
        words = (c[..., 0::2] | (c[..., 1::2] << 4)).reshape(k // 512, 128, 2 * n)
    return np.ascontiguousarray(words), np.ascontiguousarray(byte.astype(np.uint8).reshape(k // 512, 16, n))


def unpack_weight(words, scales, fmt):
    g, _, n = scales.shape
    words = np.ascontiguousarray(words).reshape(g, 128, n, -1)
    if fmt == "e4m3":
        vals = words.view(ml_dtypes.float8_e4m3fn).astype(np.float64)
    else:
        nib = np.empty((g, 128, n, 4), np.uint8)
        nib[..., 0::2] = words & 0xF
        nib[..., 1::2] = words >> 4
        vals = E2M1[nib]
    vals = vals * np.repeat(np.exp2(scales.astype(np.float64) - 127.0), 8, axis=1)[..., None]
    return vals.transpose(0, 1, 3, 2).reshape(g * 512, n)


def gelu(v):
    return 0.5 * v * (1.0 + np.tanh(np.sqrt(2.0 / np.pi) * (v + 0.044715 * v**3)))


K, K2, H, N, T, S, T2, P = 1024, 1536, 1024, 512, 2048, 512, 2048, 1024

def setup_inputs():
    n = np.random.standard_normal
    s, s2, u = mx_kscale(K)[:, None], mx_kscale(K2)[:, None], mx_kscale(H)[:, None]
    perm = np.random.permutation(T2)
    d = {}
    d["tab_words"], d["tab_scales"] = pack_weight(n((K, T)) * s, "e4m3")
    d["tab2_words"], d["tab2_scales"] = pack_weight(n((K2, T)) * s2, "e4m3")
    d["offs"] = striped(np.random.permutation(T)[:S])
    d["offs2"] = striped(np.random.permutation(T)[:S])
    d["offs3"] = striped(perm[:S])
    d["offs4"] = striped(perm[S:2 * S])
    d["offs5"] = striped(np.random.permutation(T2)[:P])
    d["w1"] = (1.3 * n((K, H)) / K**0.5 / s).astype(np.float32)
    d["w2_words"], d["w2_scales"] = pack_weight(0.55 * n((K2, H)) / K2**0.5 / s2, "e2m1")
    d["w3"] = (n((H, N)) / H**0.5 / u).astype(np.float32)
    d["wg1"] = (1.4 * np.exp(0.3 * n((128, S)))).astype(np.float32)
    d["wg2"] = (1.4 * np.exp(0.3 * n((128, S)))).astype(np.float32)
    d["page0"] = (0.4 * n((H, T2))).astype(np.float32)
    d["plan"] = (0.35 * n((H, P))).astype(np.float32)
    d["gain"] = (1.5 * np.exp(0.3 * n(H)) * u[:, 0]).astype(np.float32)
    return d

def reference(tab_words, tab_scales, tab2_words, tab2_scales, offs, offs2, offs3, offs4, offs5,
              w1, w2_words, w2_scales, w3, wg1, wg2, page0, plan, gain):
    v = unpack_weight(tab_words, tab_scales, "e4m3")[:, unstriped(offs)]
    v2 = unpack_weight(tab2_words, tab2_scales, "e4m3")[:, unstriped(offs2)]
    a = mxq(f64(w1), 0, "e4m3").T @ v
    b = unpack_weight(w2_words, w2_scales, "e2m1").T @ v2
    h1 = a / (1.0 + a * a)
    h2 = b * np.sin(b)
    page = f64(page0).copy()
    page[:, unstriped(offs3)] = np.tile(f64(wg1), (H // 128, 1)) * h1
    page[:, unstriped(offs4)] = np.tile(f64(wg2), (H // 128, 1)) * h2
    x = (page[:, unstriped(offs5)] - f64(plan)) * f64(gain)[:, None]
    return mxq(f64(w3), 0, "e4m3").T @ mxq(x, 0, "e4m3")

@@ -1,0 +1,356 @@
+import math
+from contextlib import ExitStack
+
+import concourse.mybir as mybir
+
+K, K2, H, N, T, S, T2, PJ = 1024, 1536, 1024, 512, 2048, 512, 2048, 1024
+FLOPS = 2 * (K * H * S + K2 * H * S + H * N * PJ)
+
+F32 = mybir.dt.float32
+BF16 = mybir.dt.bfloat16
+I32 = mybir.dt.int32
+U32 = mybir.dt.uint32
+U16 = mybir.dt.uint16
+U8 = mybir.dt.uint8
+FP8X4 = mybir.dt.float8_e4m3fn_x4
+FP4X4 = mybir.dt.float4_e2m1fn_x4
+ACT = mybir.ActivationFunctionType
+ALU = mybir.AluOpType
+
+P = 128
+PACK = 4
+KP = P * PACK
+CHUNK = 256
+TWO_PI = 2.0 * math.pi
+
+
+def tile_list_aligner_stage_slots_kernel(
+    tc, tab_words, tab_scales, tab2_words, tab2_scales, offs, offs2, offs3, offs4, offs5,
+    w1, w2_words, w2_scales, w3, wg1, wg2, page0, plan, gain, out,
+):
+    nc = tc.nc
+    with ExitStack() as ctx:
+        keep = ctx.enter_context(tc.tile_pool(name="keep", bufs=1))
+        ring = ctx.enter_context(tc.tile_pool(name="ring", bufs=4))
+        work = ctx.enter_context(tc.tile_pool(name="work", bufs=2))
+        psum = ctx.enter_context(tc.psum_pool(name="psum", bufs=4))
+
+        def load_list(src, name):
+            tile = keep.tile([P, src.shape[1]], U16, name=name)
+            nc.sync.dma_start(tile[:], src)
+            return tile
+
+        def zeroed_plane(engine, width, name):
+            tile = keep.tile([P, width], U8, name=name, align_bytes=64)
+            engine.memset(tile[:].bitcast(I32), 0)
+            return tile
+
+        def load_scale_rows(queue, tile, scales):
+            passes = scales.shape[0]
+            for q in range(4):
+                queue.dma_start(
+                    out=tile[32 * q : 32 * q + 4 * passes, :].bitcast(I32),
+                    in_=scales[:, 4 * q : 4 * q + 4, :].bitcast(I32),
+                )
+
+        def lowered_plane(packed, target, a):
+            nc.gpsimd.dma_start(out=target[0:112, :].bitcast(I32), in_=packed[4 * a : 4 * a + 112, :].bitcast(I32))
+
+        def load_words(words, a, name):
+            tile = ring.tile([P, T], I32, name=name, tag="ring", align_bytes=64)
+            nc.sync.dma_start(out=tile[:], in_=words[a].rearrange("p t i -> p (t i)").bitcast(I32))
+            return tile
+
+        def gather_words(table, lst, name):
+            tile = keep.tile([P, S], U32, name=name, align_bytes=64)
+            nc.vector.tensor_copy(tile[:], table[:].bitcast(U32).indirect(lst[:]))
+            return tile
+
+        def gather_bytes(table, lst, name):
+            tile = keep.tile([P, S], U8, name=name, align_bytes=64)
+            nc.vector.tensor_copy(tile[:], table[:].indirect(lst[:]))
+            return tile
+
+        def load_page(s):
+            b, t = divmod(s, PACK)
+            tile = keep.tile([P, T2], F32, name="page%d" % s)
+            rows = page0[b * KP : (b + 1) * KP, :].rearrange("(p t) c -> p t c", t=PACK)
+            nc.sync.dma_start(out=tile[:], in_=rows[:, t, :])
+            return tile
+
+        def load_gate(wg, name):
+            tile = keep.tile([P, PACK * S], F32, name=name)
+            for q in range(4):
+                nc.sync.dma_start(out=tile[32 * q : 32 * q + 32, :], in_=wg.rearrange("(q t) j -> q (t j)", t=PACK))
+            return tile
+
+        def load_weight(w, a, c0, name):
+            tile = ring.tile([P, PACK, 512], F32, name=name, tag="ring", align_bytes=64)
+            rows = w[a * KP : (a + 1) * KP, c0 : c0 + 512]
+            nc.sync.dma_start(out=tile[:], in_=rows.rearrange("(p i) c -> p i c", i=PACK))
+            return tile
+
+        def quantize(grouped, codes, scales):
+            nc.vector.quantize_mx(out=codes.bitcast(FP8X4), scales=scales, in_=grouped)
+
+        def quantize_w1(raw, name, lodged=None):
+            if lodged is None:
+                grouped = work.tile([P, 2048], BF16, name="grouped", tag="grouped", align_bytes=64)
+            else:
+                grouped = keep.tile([P, 2048], BF16, name="grouped", tag=lodged, align_bytes=64)
+            nc.scalar.copy(
+                out=grouped[:].rearrange("p (t m i) -> p m t i", t=PACK, i=PACK),
+                in_=raw[:].rearrange("p i (m t) -> p m t i", t=PACK),
+            )
+            codes = keep.tile([P, 512], U32, name=name + "c", tag=name, align_bytes=64)
+            scales = keep.tile([P, 512], U8, name=name + "s", align_bytes=64)
+            quantize(grouped[:], codes[:], scales[:])
+            return codes, scales
+
+        def quantize_w3(raw, name):
+            grouped = work.tile([P, 2048], BF16, name="grouped", tag="grouped", align_bytes=64)
+            nc.scalar.copy(
+                out=grouped[:].rearrange("p (n i) -> p n i", i=PACK),
+                in_=raw[:].rearrange("p i n -> p n i"),
+            )
+            codes = keep.tile([P, 512], U32, name=name + "c", tag=name, align_bytes=64)
+            scales = keep.tile([P, 512], U8, name=name + "s", align_bytes=64)
+            quantize(grouped[:], codes[:], scales[:])
+            return codes, scales
+
+        def temp(tag, dtype=F32, lodged=None):
+            if lodged is not None:
+                return keep.tile([P, S], dtype, name=tag, tag=lodged, align_bytes=64)
+            return work.tile([P, S], dtype, name=tag, tag=tag)
+
+
+        def load_w2(b):
+            tile = ring.tile([P, 3, H], U8, name="w2_raw%d" % b, tag="ring", align_bytes=64)
+            src = w2_words[:, :, b * H : (b + 1) * H].rearrange("a p c -> p a c")
+            nc.sync.dma_start(out=tile[:].bitcast(I32), in_=src.bitcast(I32))
+            return tile
+
+        def deal_w2(b):
+            dealt = keep.tile([P, 3, H], U8, name="w2_%d" % b, align_bytes=64)
+            nc.vector.tensor_copy(
+                out=dealt[:].bitcast(U16).rearrange("p a (t q) -> p a t q", t=PACK),
+                in_=w2_raw[b][:].bitcast(U16).rearrange("p a (q t) -> p a t q", t=PACK),
+            )
+            return dealt
+
+        def second_stream(s, lodged=None, sine_in=None):
+            b, t = divmod(s, PACK)
+            acc = psum.tile([P, S], F32, name="acc", tag="acc")
+            for a in range(3):
+                nc.tensor.matmul_mx(
+                    out=acc[:],
+                    lhsT=w2[b][:, a, 256 * t : 256 * (t + 1)].bitcast(FP4X4),
+                    lhsT_scale=w2s[a][:, P * s : P * (s + 1)],
+                    rhs=v2[a][:].bitcast(FP8X4),
+                    rhs_scale=v2s[a][:],
+                    start=(a == 0),
+                    stop=(a == 2),
+                )
+            mag = temp("t0")
+            nc.scalar.activation(out=mag[:], in_=acc[:], func=ACT.Abs)
+            turns = temp("t1", U32)
+            nc.scalar.activation(out=turns[:], in_=mag[:], func=ACT.Copy, scale=1.0 / TWO_PI, bias=0.6)
+            angle = temp("t2")
+            nc.vector.scalar_tensor_tensor(
+                out=angle[:], in0=turns[:].bitcast(I32), scalar=-TWO_PI, in1=mag[:], op0=ALU.mult, op1=ALU.add
+            )
+            sine = temp("t3", lodged=sine_in)
+            nc.scalar.activation(out=sine[:], in_=angle[:], func=ACT.Sin, bias=TWO_PI)
+            gated = temp("t4", lodged=lodged)
+            nc.vector.tensor_tensor(gated[:], mag[:], gate2[:, S * t : S * (t + 1)], ALU.mult)
+            nc.vector.tensor_tensor(pages[s][:].indirect(list4[:]), gated[:], sine[:], ALU.mult)
+
+        def first_stream(s, gated_in=None, inv_in=None):
+            b, t = divmod(s, PACK)
+            acc = psum.tile([P, S], F32, name="acc", tag="acc")
+            for a in range(2):
+                codes, scales = w1q[a, b]
+                nc.tensor.matmul_mx(
+                    out=acc[:],
+                    lhsT=codes[:, P * t : P * (t + 1)].bitcast(FP8X4),
+                    lhsT_scale=scales[:, P * t : P * (t + 1)],
+                    rhs=v[a][:].bitcast(FP8X4),
+                    rhs_scale=vs[4 * a : P, :],
+                    start=(a == 0),
+                    stop=(a == 1),
+                )
+            sq = temp("t0")
+            nc.scalar.activation(out=sq[:], in_=acc[:], func=ACT.Square)
+            den2 = temp("t1")
+            nc.scalar.activation(out=den2[:], in_=sq[:], func=ACT.Square, bias=1.0)
+            inv = temp("t3", lodged=inv_in)
+            nc.scalar.activation(out=inv[:], in_=den2[:], func=ACT.Abs_reciprocal_sqrt)
+            gated = temp("t4", lodged=gated_in)
+            nc.vector.tensor_tensor(gated[:], acc[:], gate1[:, S * t : S * (t + 1)], ALU.mult)
+            nc.vector.tensor_tensor(pages[s][:].indirect(list3[:]), gated[:], inv[:], ALU.mult)
+
+        def deviation(s, j0, width, rounded):
+            b, t = divmod(s, PACK)
+            diff = work.tile([P, width], F32, name="diff", tag="diff", bufs=3)
+            nc.vector.tensor_tensor(
+                diff[:],
+                pages[s][:].indirect(list5[:, j0 // 16 : (j0 + width) // 16]),
+                plans[s][:, j0 : j0 + width],
+                ALU.subtract,
+            )
+            nc.scalar.activation(out=rounded, in_=diff[:], func=ACT.Copy, scale=gains[:, b, t : t + 1])
+
+        def weave_views(rows, width):
+            grouped = work.tile([P, PACK * width], BF16, name="grouped", tag="grouped", align_bytes=64)
+            dst = grouped[:].rearrange("p (c i t) -> p c t i", i=4, t=PACK)
+            src = rows.rearrange("p t (c i) -> p c t i", i=4)
+            return grouped, dst, src
+
+        def load_plan(u):
+            b, h = divmod(u, 2)
+            tile = ring.tile([P, 2, PJ], F32, name="plan%d" % u, tag="ring", align_bytes=64)
+            rows = plan[b * KP : (b + 1) * KP, :].rearrange("(p t) j -> p t j", t=PACK)
+            nc.sync.dma_start(out=tile[:], in_=rows[:, 2 * h : 2 * h + 2, :])
+            return tile
+
+        def load_plan_slice(t):
+            tile = keep.tile([P, PJ], F32, name="plan_s%d" % t, tag="plan_s%d" % t, align_bytes=64)
+            nc.sync.dma_start(out=tile[:], in_=plan[0:KP, :].rearrange("(p t) j -> p t j", t=PACK)[:, t, :])
+            return tile[:]
+
+        xrows = keep.tile([P, PACK, PJ], BF16, name="xrows")
+        w3q = []
+        x0 = []
+
+        def quantize_x0(h):
+            grouped, dst, src = weave_views(xrows[:, :, 512 * h : 512 * (h + 1)], 512)
+            nc.scalar.copy(out=dst, in_=src)
+            codes = keep.tile([P, 512], U32, name="x0c%d" % h, tag="x0c%d" % h, align_bytes=64)
+            scales = keep.tile([P, 512], U8, name="x0s%d" % h, align_bytes=64)
+            quantize(grouped[:], codes[:], scales[:])
+            x0.append((codes, scales))
+
+
+        warm_in = keep.tile([P, 1], F32, name="warm_in")
+        warm_out = keep.tile([P, 1], F32, name="warm_out")
+        nc.vector.memset(warm_in[:], 1.0)
+        nc.scalar.activation(out=warm_out[:], in_=warm_in[:], func=ACT.Abs_reciprocal_sqrt)
+        ts_raw = zeroed_plane(nc.gpsimd, T, "ts_raw")
+        t2s_raw = zeroed_plane(nc.vector, T, "t2s_raw")
+        w2s_raw = zeroed_plane(nc.vector, H, "w2s_raw")
+        v2s_low = [zeroed_plane(nc.vector, S, "v2s%d" % a) for a in (1, 2)]
+        w2s_low = [zeroed_plane(nc.vector, H, "w2s%d" % a) for a in (1, 2)]
+
+        list1 = load_list(offs, "list1")
+        raw00 = load_weight(w1, 0, 0, "w1_00")
+        load_scale_rows(nc.sync, ts_raw, tab_scales)
+        raw10 = load_weight(w1, 1, 0, "w1_10")
+        tab = [load_words(tab_words, a, "tab_%d" % a) for a in range(2)]
+        gate1 = load_gate(wg1, "gate1")
+        list3 = load_list(offs3, "list3")
+        pages = [load_page(0), load_page(1)]
+        list2 = load_list(offs2, "list2")
+        load_scale_rows(nc.sync, t2s_raw, tab2_scales)
+        load_scale_rows(nc.sync, w2s_raw, w2_scales)
+
+        w1q = {}
+        vs = gather_bytes(ts_raw, list1, "vs")
+        w1q[0, 0] = quantize_w1(raw00, "w1q00")
+        w1q[1, 0] = quantize_w1(raw10, "w1q10")
+        v = [gather_words(tab[a], list1, "v_%d" % a) for a in range(2)]
+
+        raw01 = load_weight(w1, 0, 512, "w1_01")
+        pages.append(load_page(2))
+        raw11 = load_weight(w1, 1, 512, "w1_11")
+        pages.append(load_page(3))
+        w2_raw = [load_w2(0), load_w2(1)]
+        pages.append(load_page(4))
+
+        first_stream(0)
+        v2s = [gather_bytes(t2s_raw, list2, "v2s0")] + v2s_low
+        first_stream(1, "w1q01")
+        w2s = [keep.tile([P, H], U8, name="w2s0", align_bytes=64)] + w2s_low
+        nc.vector.tensor_copy(
+            out=w2s[0][:].rearrange("p (b t q) -> p b t q", b=2, t=PACK),
+            in_=w2s_raw[:].rearrange("p (b q t) -> p b t q", b=2, t=PACK),
+        )
+        for a in (1, 2):
+            lowered_plane(v2s[0], v2s[a], a)
+        for a in (1, 2):
+            lowered_plane(w2s[0], w2s[a], a)
+        w1q[0, 1] = quantize_w1(raw01, "w1q01")
+        first_stream(2, "w1q11")
+        w1q[1, 1] = quantize_w1(raw11, "w1q11")
+
+        tab2 = [load_words(tab2_words, 0, "tab2_0")]
+        pages.append(load_page(5))
+        tab2.append(load_words(tab2_words, 1, "tab2_1"))
+        tab2.append(load_words(tab2_words, 2, "tab2_2"))
+        pages.append(load_page(6))
+        pages.append(load_page(7))
+        gate2 = load_gate(wg2, "gate2")
+        list4 = load_list(offs4, "list4")
+        list5 = load_list(offs5, "list5")
+        gains = keep.tile([P, 2, PACK], F32, name="gains")
+        nc.sync.dma_start(out=gains[:], in_=gain.rearrange("(b p t) -> p b t", b=2, t=PACK))
+        plans = [load_plan_slice(t) for t in range(PACK)]
+
+        first_stream(3)
+        w2 = [deal_w2(0), deal_w2(1)]
+        first_stream(4)
+        v2 = [gather_words(tab2[0], list2, "v2_0")]
+        first_stream(5)
+        v2.append(gather_words(tab2[1], list2, "v2_1"))
+        v2.append(gather_words(tab2[2], list2, "v2_2"))
+        first_stream(6)
+        first_stream(7)
+
+        raw3 = [load_weight(w3, b, 0, "w3_%d" % b) for b in range(2)]
+        late_plans = [load_plan(2), load_plan(3)]
+        plans.extend([late_plans[t // 2][:, t % 2, :] for t in range(PACK)])
+
+        second_stream(0)
+        second_stream(1, sine_in="w3q0")
+        deviation(0, 0, PJ, xrows[:, 0, :])
+        w3q.append(quantize_w3(raw3[0], "w3q0"))
+        second_stream(2, sine_in="w3q1")
+        deviation(1, 0, PJ, xrows[:, 1, :])
+        w3q.append(quantize_w3(raw3[1], "w3q1"))
+        second_stream(3, "plan_s0")
+        deviation(2, 0, PJ, xrows[:, 2, :])
+        second_stream(4, "plan_s1")
+        deviation(3, 0, PJ, xrows[:, 3, :])
+        second_stream(5, "plan_s2")
+        second_stream(6, "plan_s3", "x0c0")
+        quantize_x0(0)
+        second_stream(7, None, "x0c1")
+        quantize_x0(1)
+
+        out_view = out.rearrange("(m p) j -> p m j", p=P)
+        for j0 in range(0, PJ, CHUNK):
+            rows = work.tile([P, PACK, CHUNK], BF16, name="rows", tag="rows")
+            for t in range(PACK):
+                deviation(PACK + t, j0, CHUNK, rows[:, t, :])
+            grouped, dst, src = weave_views(rows[:], CHUNK)
+            nc.vector.tensor_copy(out=dst, in_=src)
+            x1c = work.tile([P, CHUNK], U32, name="x1c", tag="x1c", align_bytes=64)
+            x1s = work.tile([P, CHUNK], U8, name="x1s", tag="x1s", align_bytes=64)
+            quantize(grouped[:], x1c[:], x1s[:])
+            staged = ring.tile([P, 4, CHUNK], F32, name="staged", tag="ring", align_bytes=64)
+            for half in range(2):
+                bank = psum.tile([P, 2, CHUNK], F32, name="bank", tag="bank")
+                for mm in range(2):
+                    m = 2 * half + mm
+                    cols = slice(P * m, P * (m + 1))
+                    for b in range(2):
+                        nc.tensor.matmul_mx(
+                            out=bank[:, mm, :],
+                            lhsT=w3q[b][0][:, cols].bitcast(FP8X4),
+                            lhsT_scale=w3q[b][1][:, cols],
+                            rhs=(x0[j0 // 512][0][:, j0 % 512 : j0 % 512 + CHUNK] if b == 0 else x1c[:]).bitcast(FP8X4),
+                            rhs_scale=x0[j0 // 512][1][:, j0 % 512 : j0 % 512 + CHUNK] if b == 0 else x1s[:],
+                            start=(b == 0),
+                            stop=(b == 1),
+                        )
+                nc.scalar.copy(out=staged[:, 2 * half : 2 * half + 2, :], in_=bank[:])
+            nc.sync.dma_start(out=out_view[:, :, j0 : j0 + CHUNK], in_=staged[:])

@@ -181,13 +181,17 @@ def tile_list_aligner_stage_slots_kernel(
                 )
             sq = temp("t0")
             nc.scalar.activation(out=sq[:], in_=acc[:], func=ACT.Square)
+            lin = temp("t2")
+            nc.scalar.copy(out=lin[:], in_=acc[:])
             den2 = temp("t1")
             nc.scalar.activation(out=den2[:], in_=sq[:], func=ACT.Square, bias=1.0)
+            gated = temp("t5")
+            nc.gpsimd.tensor_tensor(gated[:], lin[:], gate1[:, S * t : S * (t + 1)], ALU.mult)
             inv = temp("t3", lodged=inv_in)
             nc.scalar.activation(out=inv[:], in_=den2[:], func=ACT.Abs_reciprocal_sqrt)
-            gated = temp("t4", lodged=gated_in)
-            nc.vector.tensor_tensor(gated[:], acc[:], gate1[:, S * t : S * (t + 1)], ALU.mult)
-            nc.vector.tensor_tensor(pages[s][:].indirect(list3[:]), gated[:], inv[:], ALU.mult)
+            prod = temp("t4", lodged=gated_in)
+            nc.gpsimd.tensor_tensor(prod[:], gated[:], inv[:], ALU.mult)
+            nc.vector.tensor_copy(pages[s][:].indirect(list3[:]), prod[:])
 
         def deviation(s, j0, width, rounded):
             b, t = divmod(s, PACK)

@@ -2,6 +2,7 @@ import math
 from contextlib import ExitStack
 
 import concourse.mybir as mybir
+from concourse.masks import make_identity
 
 K, K2, H, N, T, S, T2, PJ = 1024, 1536, 1024, 512, 2048, 512, 2048, 1024
 FLOPS = 2 * (K * H * S + K2 * H * S + H * N * PJ)
@@ -19,9 +20,19 @@ ALU = mybir.AluOpType
 
 P = 128
 PACK = 4
-KP = P * PACK
+PASS = P * PACK
+SLICES = H // P
+QUADRANT = 32
+LOWERED_ROWS = 112
 CHUNK = 256
+AHEAD = 2
+GATED_ON_VECTOR = 2
+ACC_BANKS = 2
 TWO_PI = 2.0 * math.pi
+
+DEPTH = {"step1": 3, "step2": 2, "step3": 2, "function": 2, "angle": 3, "gated": 3, "values": 3}
+DIFF_DEPTH = PACK
+X_DEPTH = 3
 
 
 def tile_list_aligner_stage_slots_kernel(
@@ -33,33 +44,70 @@ def tile_list_aligner_stage_slots_kernel(
         keep = ctx.enter_context(tc.tile_pool(name="keep", bufs=1))
         ring = ctx.enter_context(tc.tile_pool(name="ring", bufs=4))
         work = ctx.enter_context(tc.tile_pool(name="work", bufs=2))
-        psum = ctx.enter_context(tc.psum_pool(name="psum", bufs=4))
+        psum = ctx.enter_context(tc.psum_pool(name="psum", bufs=1))
+
 
         def load_list(src, name):
             tile = keep.tile([P, src.shape[1]], U16, name=name)
             nc.sync.dma_start(tile[:], src)
             return tile
 
-        def zeroed_plane(engine, width, name):
+        def zeroed_plane(width, name):
             tile = keep.tile([P, width], U8, name=name, align_bytes=64)
-            engine.memset(tile[:].bitcast(I32), 0)
+            nc.vector.memset(tile[:].bitcast(I32), 0)
             return tile
 
-        def load_scale_rows(queue, tile, scales):
+        def load_scale_rows(tile, scales):
             passes = scales.shape[0]
-            for q in range(4):
-                queue.dma_start(
-                    out=tile[32 * q : 32 * q + 4 * passes, :].bitcast(I32),
+            for q in range(P // QUADRANT):
+                nc.sync.dma_start(
+                    out=tile[QUADRANT * q : QUADRANT * q + 4 * passes, :].bitcast(I32),
                     in_=scales[:, 4 * q : 4 * q + 4, :].bitcast(I32),
                 )
 
-        def lowered_plane(packed, target, a):
-            nc.gpsimd.dma_start(out=target[0:112, :].bitcast(I32), in_=packed[4 * a : 4 * a + 112, :].bitcast(I32))
+        def lower_planes(planes):
+            for a in range(1, len(planes)):
+                nc.sync.dma_start(
+                    out=planes[a][0:LOWERED_ROWS, :].bitcast(I32),
+                    in_=planes[0][4 * a : 4 * a + LOWERED_ROWS, :].bitcast(I32),
+                )
 
         def load_words(words, a, name):
             tile = ring.tile([P, T], I32, name=name, tag="ring", align_bytes=64)
             nc.sync.dma_start(out=tile[:], in_=words[a].rearrange("p t i -> p (t i)").bitcast(I32))
             return tile
+
+        def load_page(s):
+            g, t = divmod(s, PACK)
+            tile = keep.tile([P, T2], F32, name="page%d" % s)
+            rows = page0[g * PASS : (g + 1) * PASS, :].rearrange("(p t) c -> p t c", t=PACK)
+            nc.sync.dma_start(out=tile[:], in_=rows[:, t, :])
+            return tile
+
+        def load_gate(wg):
+            tile = between("angle")
+            nc.sync.dma_start(out=tile[:], in_=wg)
+            return tile
+
+        def load_weight(w, a, g, name):
+            tile = ring.tile([P, PACK, PASS], F32, name=name, tag="ring", align_bytes=64)
+            rows = w[a * PASS : (a + 1) * PASS, g * PASS : (g + 1) * PASS]
+            nc.sync.dma_start(out=tile[:], in_=rows.rearrange("(p i) c -> p i c", i=PACK))
+            return tile
+
+        def load_plan(g, h, pool, tag):
+            tile = pool.tile([P, PACK, PJ // 2], F32, name="plan%d%d" % (g, h), tag=tag, align_bytes=64)
+            rows = plan[g * PASS : (g + 1) * PASS, h * PJ // 2 : (h + 1) * PJ // 2]
+            nc.sync.dma_start(out=tile[:], in_=rows.rearrange("(p t) j -> p t j", t=PACK))
+            return tile
+
+        def between(kind, dtype=F32, tag=None):
+            if tag is not None:
+                return keep.tile([P, S], dtype, name=kind, tag=tag, align_bytes=64)
+            return work.tile([P, S], dtype, name=kind, tag=kind, bufs=DEPTH[kind])
+
+        def bank(shape, name):
+            return psum.tile(shape, F32, name=name, tag="bank", bufs=8 - ACC_BANKS)
 
         def gather_words(table, lst, name):
             tile = keep.tile([P, S], U32, name=name, align_bytes=64)
@@ -71,290 +119,277 @@ def tile_list_aligner_stage_slots_kernel(
             nc.vector.tensor_copy(tile[:], table[:].indirect(lst[:]))
             return tile
 
-        def load_page(s):
-            b, t = divmod(s, PACK)
-            tile = keep.tile([P, T2], F32, name="page%d" % s)
-            rows = page0[b * KP : (b + 1) * KP, :].rearrange("(p t) c -> p t c", t=PACK)
-            nc.sync.dma_start(out=tile[:], in_=rows[:, t, :])
-            return tile
+        def deal_gate(natural, name, tag):
+            blocks = S // P
+            turned = bank([P, blocks, P], "turned")
+            for jb in range(blocks):
+                nc.tensor.transpose(turned[:, jb, :], natural[:, P * jb : P * (jb + 1)], ident[:])
+            spread = keep.tile([P, blocks, PACK, P // QUADRANT, QUADRANT], F32, name="spread", tag=tag, align_bytes=64)
+            for jb in range(blocks):
+                src = turned[:, jb, :].rearrange("p (q t) -> p t q", t=PACK).unsqueeze(2)
+                nc.scalar.copy(out=spread[:, jb], in_=src.to_broadcast([P, PACK, P // QUADRANT, QUADRANT]))
+            dealt = []
+            for t in range(PACK):
+                restored = bank([P, S], "restored")
+                for jb in range(blocks):
+                    src = spread[:, jb, t].rearrange("p c q -> p (c q)")
+                    nc.tensor.transpose(restored[:, P * jb : P * (jb + 1)], src, ident[:])
+                tile = keep.tile([P, S], F32, name="%s%d" % (name, t))
+                nc.scalar.copy(out=tile[:], in_=restored[:])
+                dealt.append(tile)
+            return dealt
 
-        def load_gate(wg, name):
-            tile = keep.tile([P, PACK * S], F32, name=name)
-            for q in range(4):
-                nc.sync.dma_start(out=tile[32 * q : 32 * q + 32, :], in_=wg.rearrange("(q t) j -> q (t j)", t=PACK))
-            return tile
+        def quantize(grouped, codes, plane):
+            nc.vector.quantize_mx(out=codes[:].bitcast(FP8X4), scales=plane[:], in_=grouped[:])
+            return codes, plane
 
-        def load_weight(w, a, c0, name):
-            tile = ring.tile([P, PACK, 512], F32, name=name, tag="ring", align_bytes=64)
-            rows = w[a * KP : (a + 1) * KP, c0 : c0 + 512]
-            nc.sync.dma_start(out=tile[:], in_=rows.rearrange("(p i) c -> p i c", i=PACK))
-            return tile
+        def quantize_weight(grouped, name):
+            codes = keep.tile([P, PASS], U32, name=name + "_codes", align_bytes=64)
+            plane = keep.tile([P, PASS], U8, name=name + "_plane", align_bytes=64)
+            return quantize(grouped, codes, plane)
 
-        def quantize(grouped, codes, scales):
-            nc.vector.quantize_mx(out=codes.bitcast(FP8X4), scales=scales, in_=grouped)
-
-        def quantize_w1(raw, name, lodged=None):
-            if lodged is None:
-                grouped = work.tile([P, 2048], BF16, name="grouped", tag="grouped", align_bytes=64)
-            else:
-                grouped = keep.tile([P, 2048], BF16, name="grouped", tag=lodged, align_bytes=64)
+        def quantize_w1(raw, name):
+            grouped = work.tile([P, PACK * PASS], BF16, name="grouped", tag="grouped", align_bytes=64)
             nc.scalar.copy(
                 out=grouped[:].rearrange("p (t m i) -> p m t i", t=PACK, i=PACK),
                 in_=raw[:].rearrange("p i (m t) -> p m t i", t=PACK),
             )
-            codes = keep.tile([P, 512], U32, name=name + "c", tag=name, align_bytes=64)
-            scales = keep.tile([P, 512], U8, name=name + "s", align_bytes=64)
-            quantize(grouped[:], codes[:], scales[:])
-            return codes, scales
+            return quantize_weight(grouped, name)
 
-        def quantize_w3(raw, name):
-            grouped = work.tile([P, 2048], BF16, name="grouped", tag="grouped", align_bytes=64)
+        def quantize_w3(raw, name, tag):
+            grouped = keep.tile([P, PACK * N], BF16, name="grouped", tag=tag, align_bytes=64)
             nc.scalar.copy(
                 out=grouped[:].rearrange("p (n i) -> p n i", i=PACK),
                 in_=raw[:].rearrange("p i n -> p n i"),
             )
-            codes = keep.tile([P, 512], U32, name=name + "c", tag=name, align_bytes=64)
-            scales = keep.tile([P, 512], U8, name=name + "s", align_bytes=64)
-            quantize(grouped[:], codes[:], scales[:])
-            return codes, scales
+            return quantize_weight(grouped, name)
 
-        def temp(tag, dtype=F32, lodged=None):
-            if lodged is not None:
-                return keep.tile([P, S], dtype, name=tag, tag=lodged, align_bytes=64)
-            return work.tile([P, S], dtype, name=tag, tag=tag)
-
-
-        def load_w2(b):
-            tile = ring.tile([P, 3, H], U8, name="w2_raw%d" % b, tag="ring", align_bytes=64)
-            src = w2_words[:, :, b * H : (b + 1) * H].rearrange("a p c -> p a c")
-            nc.sync.dma_start(out=tile[:].bitcast(I32), in_=src.bitcast(I32))
-            return tile
-
-        def deal_w2(b):
-            dealt = keep.tile([P, 3, H], U8, name="w2_%d" % b, align_bytes=64)
+        def deal_w2_words(g):
+            dealt = keep.tile([P, K2 // PASS, 2 * PASS], U8, name="w2_%d" % g, align_bytes=64)
             nc.vector.tensor_copy(
-                out=dealt[:].bitcast(U16).rearrange("p a (t q) -> p a t q", t=PACK),
-                in_=w2_raw[b][:].bitcast(U16).rearrange("p a (q t) -> p a t q", t=PACK),
+                out=dealt[:].bitcast(U16).rearrange("p a (t m) -> p t a m", t=PACK),
+                in_=w2_raw[:, :, 2 * PASS * g : 2 * PASS * (g + 1)].bitcast(U16).rearrange("p a (m t) -> p t a m", t=PACK),
             )
             return dealt
 
-        def second_stream(s, lodged=None, sine_in=None):
-            b, t = divmod(s, PACK)
-            acc = psum.tile([P, S], F32, name="acc", tag="acc")
-            for a in range(3):
-                nc.tensor.matmul_mx(
-                    out=acc[:],
-                    lhsT=w2[b][:, a, 256 * t : 256 * (t + 1)].bitcast(FP4X4),
-                    lhsT_scale=w2s[a][:, P * s : P * (s + 1)],
-                    rhs=v2[a][:].bitcast(FP8X4),
-                    rhs_scale=v2s[a][:],
-                    start=(a == 0),
-                    stop=(a == 2),
-                )
-            mag = temp("t0")
-            nc.scalar.activation(out=mag[:], in_=acc[:], func=ACT.Abs)
-            turns = temp("t1", U32)
-            nc.scalar.activation(out=turns[:], in_=mag[:], func=ACT.Copy, scale=1.0 / TWO_PI, bias=0.6)
-            angle = temp("t2")
-            nc.vector.scalar_tensor_tensor(
-                out=angle[:], in0=turns[:].bitcast(I32), scalar=-TWO_PI, in1=mag[:], op0=ALU.mult, op1=ALU.add
+        def deal_w2_scales():
+            dealt = keep.tile([P, H], U8, name="w2_plane0", align_bytes=64)
+            nc.vector.tensor_copy(
+                out=dealt[:].rearrange("p (g t m) -> p g t m", t=PACK, m=P),
+                in_=w2_scales_raw[:].rearrange("p (g m t) -> p g t m", t=PACK, m=P),
             )
-            sine = temp("t3", lodged=sine_in)
-            nc.scalar.activation(out=sine[:], in_=angle[:], func=ACT.Sin, bias=TWO_PI)
-            gated = temp("t4", lodged=lodged)
-            nc.vector.tensor_tensor(gated[:], mag[:], gate2[:, S * t : S * (t + 1)], ALU.mult)
-            nc.vector.tensor_tensor(pages[s][:].indirect(list4[:]), gated[:], sine[:], ALU.mult)
+            return dealt
 
-        def first_stream(s, gated_in=None, inv_in=None):
-            b, t = divmod(s, PACK)
-            acc = psum.tile([P, S], F32, name="acc", tag="acc")
-            for a in range(2):
-                codes, scales = w1q[a, b]
+        def first_values(s):
+            g, t = divmod(s, PACK)
+            acc = psum.tile([P, S], F32, name="acc", tag="acc", bufs=ACC_BANKS)
+            passes = K // PASS
+            for a in range(passes):
+                codes, plane = w1q[a, g]
                 nc.tensor.matmul_mx(
                     out=acc[:],
                     lhsT=codes[:, P * t : P * (t + 1)].bitcast(FP8X4),
-                    lhsT_scale=scales[:, P * t : P * (t + 1)],
+                    lhsT_scale=plane[:, P * t : P * (t + 1)],
                     rhs=v[a][:].bitcast(FP8X4),
-                    rhs_scale=vs[4 * a : P, :],
+                    rhs_scale=v_planes[4 * a : P, :],
                     start=(a == 0),
-                    stop=(a == 1),
+                    stop=(a == passes - 1),
                 )
-            sq = temp("t0")
-            nc.scalar.activation(out=sq[:], in_=acc[:], func=ACT.Square)
-            lin = temp("t2")
-            nc.scalar.copy(out=lin[:], in_=acc[:])
-            den2 = temp("t1")
-            nc.scalar.activation(out=den2[:], in_=sq[:], func=ACT.Square, bias=1.0)
-            gated = temp("t5")
-            nc.gpsimd.tensor_tensor(gated[:], lin[:], gate1[:, S * t : S * (t + 1)], ALU.mult)
-            inv = temp("t3", lodged=inv_in)
-            nc.scalar.activation(out=inv[:], in_=den2[:], func=ACT.Abs_reciprocal_sqrt)
-            prod = temp("t4", lodged=gated_in)
-            nc.gpsimd.tensor_tensor(prod[:], gated[:], inv[:], ALU.mult)
-            nc.vector.tensor_copy(pages[s][:].indirect(list3[:]), prod[:])
+            square = between("step1")
+            nc.scalar.activation(out=square[:], in_=acc[:], func=ACT.Square)
+            linear = acc
+            if s >= GATED_ON_VECTOR:
+                linear = between("step3")
+                nc.scalar.copy(out=linear[:], in_=acc[:])
+            denominator = between("step2")
+            nc.scalar.activation(out=denominator[:], in_=square[:], func=ACT.Square, bias=1.0)
+            gated = between("gated")
+            gating = nc.gpsimd if s >= GATED_ON_VECTOR else nc.vector
+            gating.tensor_tensor(gated[:], linear[:], gate1[t][:], ALU.mult)
+            inverse = between("function")
+            nc.scalar.activation(out=inverse[:], in_=denominator[:], func=ACT.Abs_reciprocal_sqrt)
+            result = between("values")
+            finishing = nc.gpsimd if s > 0 else nc.vector
+            finishing.tensor_tensor(result[:], gated[:], inverse[:], ALU.mult)
+            return result
 
-        def deviation(s, j0, width, rounded):
-            b, t = divmod(s, PACK)
-            diff = work.tile([P, width], F32, name="diff", tag="diff", bufs=3)
-            nc.vector.tensor_tensor(
-                diff[:],
-                pages[s][:].indirect(list5[:, j0 // 16 : (j0 + width) // 16]),
-                plans[s][:, j0 : j0 + width],
-                ALU.subtract,
+        def second_values(s, magnitude_tag=None, back_tag=None, angle_tag=None):
+            g, t = divmod(s, PACK)
+            acc = psum.tile([P, S], F32, name="acc", tag="acc", bufs=ACC_BANKS)
+            passes = K2 // PASS
+            for a in range(passes):
+                nc.tensor.matmul_mx(
+                    out=acc[:],
+                    lhsT=w2[g][:, a, 2 * P * t : 2 * P * (t + 1)].bitcast(FP4X4),
+                    lhsT_scale=w2_planes[a][:, P * s : P * (s + 1)],
+                    rhs=v2[a][:].bitcast(FP8X4),
+                    rhs_scale=v2_planes[a][:],
+                    start=(a == 0),
+                    stop=(a == passes - 1),
+                )
+            magnitude = between("step1", tag=magnitude_tag)
+            nc.scalar.activation(out=magnitude[:], in_=acc[:], func=ACT.Abs)
+            turns = between("step2", U32)
+            nc.scalar.activation(out=turns[:], in_=magnitude[:], func=ACT.Copy, scale=1.0 / TWO_PI, bias=0.0)
+            back = between("step3", tag=back_tag)
+            nc.scalar.activation(out=back[:], in_=turns[:], func=ACT.Copy, scale=-TWO_PI, bias=0.0)
+            angle = between("angle", tag=angle_tag)
+            nc.gpsimd.tensor_tensor(angle[:], magnitude[:], back[:], ALU.add)
+            gated = between("gated")
+            nc.gpsimd.tensor_tensor(gated[:], magnitude[:], gate2[t][:], ALU.mult)
+            sine = between("function")
+            nc.scalar.activation(out=sine[:], in_=angle[:], func=ACT.Sin)
+            result = between("values")
+            nc.gpsimd.tensor_tensor(result[:], gated[:], sine[:], ALU.mult)
+            return result
+
+        def put(s, lst, values):
+            nc.vector.tensor_copy(pages[s][:].indirect(lst[:]), values[:])
+
+        def quantize_x(g, j0, rows, weave):
+            h, c0 = divmod(j0, PJ // 2)
+            for t in range(PACK):
+                diff = work.tile([P, CHUNK], F32, name="diff", tag="diff", bufs=DIFF_DEPTH)
+                nc.vector.tensor_tensor(
+                    diff[:],
+                    pages[PACK * g + t][:].indirect(list5[:, j0 // 16 : (j0 + CHUNK) // 16]),
+                    plans[g, h][:, t, c0 : c0 + CHUNK],
+                    ALU.subtract,
+                )
+                nc.scalar.activation(out=rows[:, t, :], in_=diff[:], func=ACT.Copy, scale=gains[:, g, t : t + 1])
+            grouped = work.tile([P, PACK * CHUNK], BF16, name="grouped", tag="grouped", align_bytes=64)
+            weave(
+                out=grouped[:].rearrange("p (c i t) -> p c t i", i=4, t=PACK),
+                in_=rows[:].rearrange("p t (c i) -> p c t i", i=4),
             )
-            nc.scalar.activation(out=rounded, in_=diff[:], func=ACT.Copy, scale=gains[:, b, t : t + 1])
-
-        def weave_views(rows, width):
-            grouped = work.tile([P, PACK * width], BF16, name="grouped", tag="grouped", align_bytes=64)
-            dst = grouped[:].rearrange("p (c i t) -> p c t i", i=4, t=PACK)
-            src = rows.rearrange("p t (c i) -> p c t i", i=4)
-            return grouped, dst, src
-
-        def load_plan(u):
-            b, h = divmod(u, 2)
-            tile = ring.tile([P, 2, PJ], F32, name="plan%d" % u, tag="ring", align_bytes=64)
-            rows = plan[b * KP : (b + 1) * KP, :].rearrange("(p t) j -> p t j", t=PACK)
-            nc.sync.dma_start(out=tile[:], in_=rows[:, 2 * h : 2 * h + 2, :])
-            return tile
-
-        def load_plan_slice(t):
-            tile = keep.tile([P, PJ], F32, name="plan_s%d" % t, tag="plan_s%d" % t, align_bytes=64)
-            nc.sync.dma_start(out=tile[:], in_=plan[0:KP, :].rearrange("(p t) j -> p t j", t=PACK)[:, t, :])
-            return tile[:]
-
-        xrows = keep.tile([P, PACK, PJ], BF16, name="xrows")
-        w3q = []
-        x0 = []
-
-        def quantize_x0(h):
-            grouped, dst, src = weave_views(xrows[:, :, 512 * h : 512 * (h + 1)], 512)
-            nc.scalar.copy(out=dst, in_=src)
-            codes = keep.tile([P, 512], U32, name="x0c%d" % h, tag="x0c%d" % h, align_bytes=64)
-            scales = keep.tile([P, 512], U8, name="x0s%d" % h, align_bytes=64)
-            quantize(grouped[:], codes[:], scales[:])
-            x0.append((codes, scales))
-
+            codes = work.tile([P, CHUNK], U32, name="x_codes", tag="x_codes", align_bytes=64, bufs=X_DEPTH)
+            plane = work.tile([P, CHUNK], U8, name="x_plane", tag="x_plane", align_bytes=64, bufs=X_DEPTH)
+            return quantize(grouped, codes, plane)
 
         warm_in = keep.tile([P, 1], F32, name="warm_in")
         warm_out = keep.tile([P, 1], F32, name="warm_out")
         nc.vector.memset(warm_in[:], 1.0)
         nc.scalar.activation(out=warm_out[:], in_=warm_in[:], func=ACT.Abs_reciprocal_sqrt)
-        ts_raw = zeroed_plane(nc.gpsimd, T, "ts_raw")
-        t2s_raw = zeroed_plane(nc.vector, T, "t2s_raw")
-        w2s_raw = zeroed_plane(nc.vector, H, "w2s_raw")
-        v2s_low = [zeroed_plane(nc.vector, S, "v2s%d" % a) for a in (1, 2)]
-        w2s_low = [zeroed_plane(nc.vector, H, "w2s%d" % a) for a in (1, 2)]
+        v_scales_raw = zeroed_plane(T, "v_scales_raw")
+        ident = keep.tile([P, P], F32, name="ident")
+        make_identity(nc, ident[:])
+        v2_scales_raw = zeroed_plane(T, "v2_scales_raw")
+        w2_scales_raw = zeroed_plane(H, "w2_scales_raw")
+        v2_lowered = [zeroed_plane(S, "v2_plane%d" % a) for a in range(1, K2 // PASS)]
+        w2_lowered = [zeroed_plane(H, "w2_plane%d" % a) for a in range(1, K2 // PASS)]
 
+        wg1_raw = load_gate(wg1)
+        w1_raw = {(0, 0): load_weight(w1, 0, 0, "w1_00")}
         list1 = load_list(offs, "list1")
-        raw00 = load_weight(w1, 0, 0, "w1_00")
-        load_scale_rows(nc.sync, ts_raw, tab_scales)
-        raw10 = load_weight(w1, 1, 0, "w1_10")
-        tab = [load_words(tab_words, a, "tab_%d" % a) for a in range(2)]
-        gate1 = load_gate(wg1, "gate1")
+        load_scale_rows(v_scales_raw, tab_scales)
+        gate1 = deal_gate(wg1_raw, "gate1_", "spread_then_plan0")
+        w1_raw[1, 0] = load_weight(w1, 1, 0, "w1_10")
+        tab = [load_words(tab_words, a, "tab_%d" % a) for a in range(K // PASS)]
+        w2_raw = ring.tile([P, K2 // PASS, 2 * H], U8, name="w2_raw", tag="ring", align_bytes=64)
+        nc.sync.dma_start(out=w2_raw[:].bitcast(I32), in_=w2_words.rearrange("a p c -> p a c").bitcast(I32))
+        list2 = load_list(offs2, "list2")
+        load_scale_rows(v2_scales_raw, tab2_scales)
         list3 = load_list(offs3, "list3")
         pages = [load_page(0), load_page(1)]
-        list2 = load_list(offs2, "list2")
-        load_scale_rows(nc.sync, t2s_raw, tab2_scales)
-        load_scale_rows(nc.sync, w2s_raw, w2_scales)
 
-        w1q = {}
-        vs = gather_bytes(ts_raw, list1, "vs")
-        w1q[0, 0] = quantize_w1(raw00, "w1q00")
-        w1q[1, 0] = quantize_w1(raw10, "w1q10")
-        v = [gather_words(tab[a], list1, "v_%d" % a) for a in range(2)]
+        v_planes = gather_bytes(v_scales_raw, list1, "v_planes")
+        w1q = {(a, 0): quantize_w1(w1_raw[a, 0], "w1_%d0" % a) for a in range(K // PASS)}
+        v = [gather_words(tab[a], list1, "v_%d" % a) for a in range(K // PASS)]
+        first = [first_values(0)]
 
-        raw01 = load_weight(w1, 0, 512, "w1_01")
+        w1_raw[0, 1] = load_weight(w1, 0, 1, "w1_01")
         pages.append(load_page(2))
-        raw11 = load_weight(w1, 1, 512, "w1_11")
+        w1_raw[1, 1] = load_weight(w1, 1, 1, "w1_11")
+        wg2_raw = load_gate(wg2)
+        load_scale_rows(w2_scales_raw, w2_scales)
         pages.append(load_page(3))
-        w2_raw = [load_w2(0), load_w2(1)]
+
+        first.append(first_values(1))
+        w2 = [deal_w2_words(g) for g in range(H // PASS)]
+        v2_planes = [gather_bytes(v2_scales_raw, list2, "v2_plane0")] + v2_lowered
+        first.append(first_values(2))
+        put(0, list3, first[0])
+        first.append(first_values(3))
+        put(1, list3, first[1])
+        w1q[0, 1] = quantize_w1(w1_raw[0, 1], "w1_01")
+        put(2, list3, first[2])
+        w2_planes = [deal_w2_scales()] + w2_lowered
+        w1q[1, 1] = quantize_w1(w1_raw[1, 1], "w1_11")
+        first.extend([first_values(4), first_values(5)])
+
+        tab2 = [load_words(tab2_words, a, "tab2_%d" % a) for a in range(2)]
         pages.append(load_page(4))
-
-        first_stream(0)
-        v2s = [gather_bytes(t2s_raw, list2, "v2s0")] + v2s_low
-        first_stream(1, "w1q01")
-        w2s = [keep.tile([P, H], U8, name="w2s0", align_bytes=64)] + w2s_low
-        nc.vector.tensor_copy(
-            out=w2s[0][:].rearrange("p (b t q) -> p b t q", b=2, t=PACK),
-            in_=w2s_raw[:].rearrange("p (b q t) -> p b t q", b=2, t=PACK),
-        )
-        for a in (1, 2):
-            lowered_plane(v2s[0], v2s[a], a)
-        for a in (1, 2):
-            lowered_plane(w2s[0], w2s[a], a)
-        w1q[0, 1] = quantize_w1(raw01, "w1q01")
-        first_stream(2, "w1q11")
-        w1q[1, 1] = quantize_w1(raw11, "w1q11")
-
-        tab2 = [load_words(tab2_words, 0, "tab2_0")]
-        pages.append(load_page(5))
-        tab2.append(load_words(tab2_words, 1, "tab2_1"))
+        lower_planes(v2_planes)
+        lower_planes(w2_planes)
         tab2.append(load_words(tab2_words, 2, "tab2_2"))
-        pages.append(load_page(6))
-        pages.append(load_page(7))
-        gate2 = load_gate(wg2, "gate2")
+        pages.extend([load_page(s) for s in range(5, SLICES)])
         list4 = load_list(offs4, "list4")
         list5 = load_list(offs5, "list5")
-        gains = keep.tile([P, 2, PACK], F32, name="gains")
-        nc.sync.dma_start(out=gains[:], in_=gain.rearrange("(b p t) -> p b t", b=2, t=PACK))
-        plans = [load_plan_slice(t) for t in range(PACK)]
+        gains = keep.tile([P, H // PASS, PACK], F32, name="gains")
+        nc.sync.dma_start(out=gains[:], in_=gain.rearrange("(g p t) -> p g t", p=P, t=PACK))
 
-        first_stream(3)
-        w2 = [deal_w2(0), deal_w2(1)]
-        first_stream(4)
+        put(3, list3, first[3])
+        first.append(first_values(6))
         v2 = [gather_words(tab2[0], list2, "v2_0")]
-        first_stream(5)
-        v2.append(gather_words(tab2[1], list2, "v2_1"))
-        v2.append(gather_words(tab2[2], list2, "v2_2"))
-        first_stream(6)
-        first_stream(7)
+        put(4, list3, first[4])
+        first.append(first_values(7))
+        gate2 = deal_gate(wg2_raw, "gate2_", "spread_then_plan1")
+        v2.extend([gather_words(tab2[a], list2, "v2_%d" % a) for a in range(1, K2 // PASS)])
+        put(5, list3, first[5])
+        second = []
+        for s in range(AHEAD):
+            second.append(second_values(s))
+            put(SLICES - AHEAD + s, list3, first[SLICES - AHEAD + s])
 
-        raw3 = [load_weight(w3, b, 0, "w3_%d" % b) for b in range(2)]
-        late_plans = [load_plan(2), load_plan(3)]
-        plans.extend([late_plans[t // 2][:, t % 2, :] for t in range(PACK)])
+        w3_raw = [load_weight(w3, g, 0, "w3_%d" % g) for g in range(H // PASS)]
+        plans = {(g, 0): load_plan(g, 0, keep, "spread_then_plan%d" % g) for g in range(H // PASS)}
+        for g in range(H // PASS):
+            plans[g, 1] = load_plan(g, 1, ring, "ring")
 
-        second_stream(0)
-        second_stream(1, sine_in="w3q0")
-        deviation(0, 0, PJ, xrows[:, 0, :])
-        w3q.append(quantize_w3(raw3[0], "w3q0"))
-        second_stream(2, sine_in="w3q1")
-        deviation(1, 0, PJ, xrows[:, 1, :])
-        w3q.append(quantize_w3(raw3[1], "w3q1"))
-        second_stream(3, "plan_s0")
-        deviation(2, 0, PJ, xrows[:, 2, :])
-        second_stream(4, "plan_s1")
-        deviation(3, 0, PJ, xrows[:, 3, :])
-        second_stream(5, "plan_s2")
-        second_stream(6, "plan_s3", "x0c0")
-        quantize_x0(0)
-        second_stream(7, None, "x0c1")
-        quantize_x0(1)
+        for s in range(SLICES):
+            if s + AHEAD < SLICES - 1:
+                second.append(second_values(s + AHEAD))
+            if s + AHEAD == SLICES - 1:
+                second.append(second_values(SLICES - 1, "magnitude_then_w3", "back_then_w3", "angle_then_rows"))
+            put(s, list4, second[s])
+        w3q = [
+            quantize_w3(w3_raw[0], "w3_0", "back_then_w3"),
+            quantize_w3(w3_raw[1], "w3_1", "magnitude_then_w3"),
+        ]
 
         out_view = out.rearrange("(m p) j -> p m j", p=P)
+        tiles_n, passes = N // P, H // PASS
         for j0 in range(0, PJ, CHUNK):
-            rows = work.tile([P, PACK, CHUNK], BF16, name="rows", tag="rows")
-            for t in range(PACK):
-                deviation(PACK + t, j0, CHUNK, rows[:, t, :])
-            grouped, dst, src = weave_views(rows[:], CHUNK)
-            nc.vector.tensor_copy(out=dst, in_=src)
-            x1c = work.tile([P, CHUNK], U32, name="x1c", tag="x1c", align_bytes=64)
-            x1s = work.tile([P, CHUNK], U8, name="x1s", tag="x1s", align_bytes=64)
-            quantize(grouped[:], x1c[:], x1s[:])
-            staged = ring.tile([P, 4, CHUNK], F32, name="staged", tag="ring", align_bytes=64)
-            for half in range(2):
-                bank = psum.tile([P, 2, CHUNK], F32, name="bank", tag="bank")
-                for mm in range(2):
-                    m = 2 * half + mm
-                    cols = slice(P * m, P * (m + 1))
-                    for b in range(2):
-                        nc.tensor.matmul_mx(
-                            out=bank[:, mm, :],
-                            lhsT=w3q[b][0][:, cols].bitcast(FP8X4),
-                            lhsT_scale=w3q[b][1][:, cols],
-                            rhs=(x0[j0 // 512][0][:, j0 % 512 : j0 % 512 + CHUNK] if b == 0 else x1c[:]).bitcast(FP8X4),
-                            rhs_scale=x0[j0 // 512][1][:, j0 % 512 : j0 % 512 + CHUNK] if b == 0 else x1s[:],
-                            start=(b == 0),
-                            stop=(b == 1),
-                        )
-                nc.scalar.copy(out=staged[:, 2 * half : 2 * half + 2, :], in_=bank[:])
-            nc.sync.dma_start(out=out_view[:, :, j0 : j0 + CHUNK], in_=staged[:])
+            last = j0 + CHUNK == PJ
+            xq = []
+            for g in range(passes):
+                if j0 == 0 and g == 0:
+                    rows = keep.tile([P, PACK, CHUNK], BF16, name="rows", tag="angle_then_rows", align_bytes=64)
+                else:
+                    rows = work.tile([P, PACK, CHUNK], BF16, name="rows", tag="rows", bufs=X_DEPTH)
+                xq.append(quantize_x(g, j0, rows, nc.vector.tensor_copy if last else nc.scalar.copy))
+            staged = ring.tile([P, tiles_n, CHUNK], F32, name="staged", tag="ring", align_bytes=64)
+            per_bank = 1 if last else 2
+            banks = [bank([P, per_bank, CHUNK], "sums") for k in range(tiles_n // per_bank)]
+            if last:
+                steps = [(m, g) for g in range(passes) for m in range(tiles_n)]
+            else:
+                steps = [(m, g) for m in range(tiles_n) for g in range(passes)]
+            for m, g in steps:
+                k, place = divmod(m, per_bank)
+                nc.tensor.matmul_mx(
+                    out=banks[k][:, place, :],
+                    lhsT=w3q[g][0][:, P * m : P * (m + 1)].bitcast(FP8X4),
+                    lhsT_scale=w3q[g][1][:, P * m : P * (m + 1)],
+                    rhs=xq[g][0][:].bitcast(FP8X4),
+                    rhs_scale=xq[g][1][:],
+                    start=(g == 0),
+                    stop=(g == passes - 1),
+                )
+                if g == passes - 1 and place == per_bank - 1:
+                    copy = nc.vector.tensor_copy if last and k % 2 == 1 else nc.scalar.copy
+                    copy(out=staged[:, per_bank * k : per_bank * (k + 1), :], in_=banks[k][:])
+                if last and g == passes - 1 and m % 2 == 1:
+                    nc.sync.dma_start(out=out_view[:, m - 1 : m + 1, j0 : j0 + CHUNK], in_=staged[:, m - 1 : m + 1, :])
+            if not last:
+                nc.sync.dma_start(out=out_view[:, :, j0 : j0 + CHUNK], in_=staged[:])

import math
from contextlib import ExitStack

import concourse.mybir as mybir
from concourse.masks import make_identity

K, K2, H, N, T, S, T2, PJ = 1024, 1536, 1024, 512, 2048, 512, 2048, 1024
FLOPS = 2 * (K * H * S + K2 * H * S + H * N * PJ)

F32 = mybir.dt.float32
BF16 = mybir.dt.bfloat16
I32 = mybir.dt.int32
U32 = mybir.dt.uint32
U16 = mybir.dt.uint16
U8 = mybir.dt.uint8
FP8X4 = mybir.dt.float8_e4m3fn_x4
FP4X4 = mybir.dt.float4_e2m1fn_x4
ACT = mybir.ActivationFunctionType
ALU = mybir.AluOpType

P = 128
PACK = 4
PASS = P * PACK
SLICES = H // P
QUADRANT = 32
LOWERED_ROWS = 112
CHUNK = 256
AHEAD = 2
GATED_ON_VECTOR = 2
ACC_BANKS = 2
TWO_PI = 2.0 * math.pi

DEPTH = {"step1": 3, "step2": 2, "step3": 2, "function": 2, "angle": 3, "gated": 3, "values": 3}
DIFF_DEPTH = PACK
X_DEPTH = 3


def tile_list_aligner_stage_slots_kernel(
    tc, tab_words, tab_scales, tab2_words, tab2_scales, offs, offs2, offs3, offs4, offs5,
    w1, w2_words, w2_scales, w3, wg1, wg2, page0, plan, gain, out,
):
    nc = tc.nc
    with ExitStack() as ctx:
        keep = ctx.enter_context(tc.tile_pool(name="keep", bufs=1))
        ring = ctx.enter_context(tc.tile_pool(name="ring", bufs=4))
        work = ctx.enter_context(tc.tile_pool(name="work", bufs=2))
        psum = ctx.enter_context(tc.psum_pool(name="psum", bufs=1))


        def load_list(src, name):
            tile = keep.tile([P, src.shape[1]], U16, name=name)
            nc.sync.dma_start(tile[:], src)
            return tile

        def zeroed_plane(width, name):
            tile = keep.tile([P, width], U8, name=name, align_bytes=64)
            nc.vector.memset(tile[:].bitcast(I32), 0)
            return tile

        def load_scale_rows(tile, scales):
            passes = scales.shape[0]
            for q in range(P // QUADRANT):
                nc.sync.dma_start(
                    out=tile[QUADRANT * q : QUADRANT * q + 4 * passes, :].bitcast(I32),
                    in_=scales[:, 4 * q : 4 * q + 4, :].bitcast(I32),
                )

        def lower_planes(planes):
            for a in range(1, len(planes)):
                nc.sync.dma_start(
                    out=planes[a][0:LOWERED_ROWS, :].bitcast(I32),
                    in_=planes[0][4 * a : 4 * a + LOWERED_ROWS, :].bitcast(I32),
                )

        def load_words(words, a, name):
            tile = ring.tile([P, T], I32, name=name, tag="ring", align_bytes=64)
            nc.sync.dma_start(out=tile[:], in_=words[a].rearrange("p t i -> p (t i)").bitcast(I32))
            return tile

        def load_page(s):
            g, t = divmod(s, PACK)
            tile = keep.tile([P, T2], F32, name="page%d" % s)
            rows = page0[g * PASS : (g + 1) * PASS, :].rearrange("(p t) c -> p t c", t=PACK)
            nc.sync.dma_start(out=tile[:], in_=rows[:, t, :])
            return tile

        def load_gate(wg):
            tile = between("angle")
            nc.sync.dma_start(out=tile[:], in_=wg)
            return tile

        def load_weight(w, a, g, name):
            tile = ring.tile([P, PACK, PASS], F32, name=name, tag="ring", align_bytes=64)
            rows = w[a * PASS : (a + 1) * PASS, g * PASS : (g + 1) * PASS]
            nc.sync.dma_start(out=tile[:], in_=rows.rearrange("(p i) c -> p i c", i=PACK))
            return tile

        def load_plan(g, h, pool, tag):
            tile = pool.tile([P, PACK, PJ // 2], F32, name="plan%d%d" % (g, h), tag=tag, align_bytes=64)
            rows = plan[g * PASS : (g + 1) * PASS, h * PJ // 2 : (h + 1) * PJ // 2]
            nc.sync.dma_start(out=tile[:], in_=rows.rearrange("(p t) j -> p t j", t=PACK))
            return tile

        def between(kind, dtype=F32, tag=None):
            if tag is not None:
                return keep.tile([P, S], dtype, name=kind, tag=tag, align_bytes=64)
            return work.tile([P, S], dtype, name=kind, tag=kind, bufs=DEPTH[kind])

        def bank(shape, name):
            return psum.tile(shape, F32, name=name, tag="bank", bufs=8 - ACC_BANKS)

        def gather_words(table, lst, name):
            tile = keep.tile([P, S], U32, name=name, align_bytes=64)
            nc.vector.tensor_copy(tile[:], table[:].bitcast(U32).indirect(lst[:]))
            return tile

        def gather_bytes(table, lst, name):
            tile = keep.tile([P, S], U8, name=name, align_bytes=64)
            nc.vector.tensor_copy(tile[:], table[:].indirect(lst[:]))
            return tile

        def deal_gate(natural, name, tag):
            blocks = S // P
            turned = bank([P, blocks, P], "turned")
            for jb in range(blocks):
                nc.tensor.transpose(turned[:, jb, :], natural[:, P * jb : P * (jb + 1)], ident[:])
            spread = keep.tile([P, blocks, PACK, P // QUADRANT, QUADRANT], F32, name="spread", tag=tag, align_bytes=64)
            for jb in range(blocks):
                src = turned[:, jb, :].rearrange("p (q t) -> p t q", t=PACK).unsqueeze(2)
                nc.scalar.copy(out=spread[:, jb], in_=src.to_broadcast([P, PACK, P // QUADRANT, QUADRANT]))
            dealt = []
            for t in range(PACK):
                restored = bank([P, S], "restored")
                for jb in range(blocks):
                    src = spread[:, jb, t].rearrange("p c q -> p (c q)")
                    nc.tensor.transpose(restored[:, P * jb : P * (jb + 1)], src, ident[:])
                tile = keep.tile([P, S], F32, name="%s%d" % (name, t))
                nc.scalar.copy(out=tile[:], in_=restored[:])
                dealt.append(tile)
            return dealt

        def quantize(grouped, codes, plane):
            nc.vector.quantize_mx(out=codes[:].bitcast(FP8X4), scales=plane[:], in_=grouped[:])
            return codes, plane

        def quantize_weight(grouped, name):
            codes = keep.tile([P, PASS], U32, name=name + "_codes", align_bytes=64)
            plane = keep.tile([P, PASS], U8, name=name + "_plane", align_bytes=64)
            return quantize(grouped, codes, plane)

        def quantize_w1(raw, name):
            grouped = work.tile([P, PACK * PASS], BF16, name="grouped", tag="grouped", align_bytes=64)
            nc.scalar.copy(
                out=grouped[:].rearrange("p (t m i) -> p m t i", t=PACK, i=PACK),
                in_=raw[:].rearrange("p i (m t) -> p m t i", t=PACK),
            )
            return quantize_weight(grouped, name)

        def quantize_w3(raw, name, tag):
            grouped = keep.tile([P, PACK * N], BF16, name="grouped", tag=tag, align_bytes=64)
            nc.scalar.copy(
                out=grouped[:].rearrange("p (n i) -> p n i", i=PACK),
                in_=raw[:].rearrange("p i n -> p n i"),
            )
            return quantize_weight(grouped, name)

        def deal_w2_words(g):
            dealt = keep.tile([P, K2 // PASS, 2 * PASS], U8, name="w2_%d" % g, align_bytes=64)
            nc.vector.tensor_copy(
                out=dealt[:].bitcast(U16).rearrange("p a (t m) -> p t a m", t=PACK),
                in_=w2_raw[:, :, 2 * PASS * g : 2 * PASS * (g + 1)].bitcast(U16).rearrange("p a (m t) -> p t a m", t=PACK),
            )
            return dealt

        def deal_w2_scales():
            dealt = keep.tile([P, H], U8, name="w2_plane0", align_bytes=64)
            nc.vector.tensor_copy(
                out=dealt[:].rearrange("p (g t m) -> p g t m", t=PACK, m=P),
                in_=w2_scales_raw[:].rearrange("p (g m t) -> p g t m", t=PACK, m=P),
            )
            return dealt

        def first_values(s):
            g, t = divmod(s, PACK)
            acc = psum.tile([P, S], F32, name="acc", tag="acc", bufs=ACC_BANKS)
            passes = K // PASS
            for a in range(passes):
                codes, plane = w1q[a, g]
                nc.tensor.matmul_mx(
                    out=acc[:],
                    lhsT=codes[:, P * t : P * (t + 1)].bitcast(FP8X4),
                    lhsT_scale=plane[:, P * t : P * (t + 1)],
                    rhs=v[a][:].bitcast(FP8X4),
                    rhs_scale=v_planes[4 * a : P, :],
                    start=(a == 0),
                    stop=(a == passes - 1),
                )
            square = between("step1")
            nc.scalar.activation(out=square[:], in_=acc[:], func=ACT.Square)
            linear = acc
            if s >= GATED_ON_VECTOR:
                linear = between("step3")
                nc.scalar.copy(out=linear[:], in_=acc[:])
            denominator = between("step2")
            nc.scalar.activation(out=denominator[:], in_=square[:], func=ACT.Square, bias=1.0)
            gated = between("gated")
            gating = nc.gpsimd if s >= GATED_ON_VECTOR else nc.vector
            gating.tensor_tensor(gated[:], linear[:], gate1[t][:], ALU.mult)
            inverse = between("function")
            nc.scalar.activation(out=inverse[:], in_=denominator[:], func=ACT.Abs_reciprocal_sqrt)
            result = between("values")
            finishing = nc.gpsimd if s > 0 else nc.vector
            finishing.tensor_tensor(result[:], gated[:], inverse[:], ALU.mult)
            return result

        def second_values(s, magnitude_tag=None, back_tag=None, angle_tag=None):
            g, t = divmod(s, PACK)
            acc = psum.tile([P, S], F32, name="acc", tag="acc", bufs=ACC_BANKS)
            passes = K2 // PASS
            for a in range(passes):
                nc.tensor.matmul_mx(
                    out=acc[:],
                    lhsT=w2[g][:, a, 2 * P * t : 2 * P * (t + 1)].bitcast(FP4X4),
                    lhsT_scale=w2_planes[a][:, P * s : P * (s + 1)],
                    rhs=v2[a][:].bitcast(FP8X4),
                    rhs_scale=v2_planes[a][:],
                    start=(a == 0),
                    stop=(a == passes - 1),
                )
            magnitude = between("step1", tag=magnitude_tag)
            nc.scalar.activation(out=magnitude[:], in_=acc[:], func=ACT.Abs)
            turns = between("step2", U32)
            nc.scalar.activation(out=turns[:], in_=magnitude[:], func=ACT.Copy, scale=1.0 / TWO_PI, bias=0.0)
            back = between("step3", tag=back_tag)
            nc.scalar.activation(out=back[:], in_=turns[:], func=ACT.Copy, scale=-TWO_PI, bias=0.0)
            angle = between("angle", tag=angle_tag)
            nc.gpsimd.tensor_tensor(angle[:], magnitude[:], back[:], ALU.add)
            gated = between("gated")
            nc.gpsimd.tensor_tensor(gated[:], magnitude[:], gate2[t][:], ALU.mult)
            sine = between("function")
            nc.scalar.activation(out=sine[:], in_=angle[:], func=ACT.Sin)
            result = between("values")
            nc.gpsimd.tensor_tensor(result[:], gated[:], sine[:], ALU.mult)
            return result

        def put(s, lst, values):
            nc.vector.tensor_copy(pages[s][:].indirect(lst[:]), values[:])

        def quantize_x(g, j0, rows, weave):
            h, c0 = divmod(j0, PJ // 2)
            for t in range(PACK):
                diff = work.tile([P, CHUNK], F32, name="diff", tag="diff", bufs=DIFF_DEPTH)
                nc.vector.tensor_tensor(
                    diff[:],
                    pages[PACK * g + t][:].indirect(list5[:, j0 // 16 : (j0 + CHUNK) // 16]),
                    plans[g, h][:, t, c0 : c0 + CHUNK],
                    ALU.subtract,
                )
                nc.scalar.activation(out=rows[:, t, :], in_=diff[:], func=ACT.Copy, scale=gains[:, g, t : t + 1])
            grouped = work.tile([P, PACK * CHUNK], BF16, name="grouped", tag="grouped", align_bytes=64)
            weave(
                out=grouped[:].rearrange("p (c i t) -> p c t i", i=4, t=PACK),
                in_=rows[:].rearrange("p t (c i) -> p c t i", i=4),
            )
            codes = work.tile([P, CHUNK], U32, name="x_codes", tag="x_codes", align_bytes=64, bufs=X_DEPTH)
            plane = work.tile([P, CHUNK], U8, name="x_plane", tag="x_plane", align_bytes=64, bufs=X_DEPTH)
            return quantize(grouped, codes, plane)

        warm_in = keep.tile([P, 1], F32, name="warm_in")
        warm_out = keep.tile([P, 1], F32, name="warm_out")
        nc.vector.memset(warm_in[:], 1.0)
        nc.scalar.activation(out=warm_out[:], in_=warm_in[:], func=ACT.Abs_reciprocal_sqrt)
        v_scales_raw = zeroed_plane(T, "v_scales_raw")
        ident = keep.tile([P, P], F32, name="ident")
        make_identity(nc, ident[:])
        v2_scales_raw = zeroed_plane(T, "v2_scales_raw")
        w2_scales_raw = zeroed_plane(H, "w2_scales_raw")
        v2_lowered = [zeroed_plane(S, "v2_plane%d" % a) for a in range(1, K2 // PASS)]
        w2_lowered = [zeroed_plane(H, "w2_plane%d" % a) for a in range(1, K2 // PASS)]

        wg1_raw = load_gate(wg1)
        w1_raw = {(0, 0): load_weight(w1, 0, 0, "w1_00")}
        list1 = load_list(offs, "list1")
        load_scale_rows(v_scales_raw, tab_scales)
        gate1 = deal_gate(wg1_raw, "gate1_", "spread_then_plan0")
        w1_raw[1, 0] = load_weight(w1, 1, 0, "w1_10")
        tab = [load_words(tab_words, a, "tab_%d" % a) for a in range(K // PASS)]
        w2_raw = ring.tile([P, K2 // PASS, 2 * H], U8, name="w2_raw", tag="ring", align_bytes=64)
        nc.sync.dma_start(out=w2_raw[:].bitcast(I32), in_=w2_words.rearrange("a p c -> p a c").bitcast(I32))
        list2 = load_list(offs2, "list2")
        load_scale_rows(v2_scales_raw, tab2_scales)
        list3 = load_list(offs3, "list3")
        pages = [load_page(0), load_page(1)]

        v_planes = gather_bytes(v_scales_raw, list1, "v_planes")
        w1q = {(a, 0): quantize_w1(w1_raw[a, 0], "w1_%d0" % a) for a in range(K // PASS)}
        v = [gather_words(tab[a], list1, "v_%d" % a) for a in range(K // PASS)]
        first = [first_values(0)]

        w1_raw[0, 1] = load_weight(w1, 0, 1, "w1_01")
        pages.append(load_page(2))
        w1_raw[1, 1] = load_weight(w1, 1, 1, "w1_11")
        wg2_raw = load_gate(wg2)
        load_scale_rows(w2_scales_raw, w2_scales)
        pages.append(load_page(3))

        first.append(first_values(1))
        w2 = [deal_w2_words(g) for g in range(H // PASS)]
        v2_planes = [gather_bytes(v2_scales_raw, list2, "v2_plane0")] + v2_lowered
        first.append(first_values(2))
        put(0, list3, first[0])
        first.append(first_values(3))
        put(1, list3, first[1])
        w1q[0, 1] = quantize_w1(w1_raw[0, 1], "w1_01")
        put(2, list3, first[2])
        w2_planes = [deal_w2_scales()] + w2_lowered
        w1q[1, 1] = quantize_w1(w1_raw[1, 1], "w1_11")
        first.extend([first_values(4), first_values(5)])

        tab2 = [load_words(tab2_words, a, "tab2_%d" % a) for a in range(2)]
        pages.append(load_page(4))
        lower_planes(v2_planes)
        lower_planes(w2_planes)
        tab2.append(load_words(tab2_words, 2, "tab2_2"))
        pages.extend([load_page(s) for s in range(5, SLICES)])
        list4 = load_list(offs4, "list4")
        list5 = load_list(offs5, "list5")
        gains = keep.tile([P, H // PASS, PACK], F32, name="gains")
        nc.sync.dma_start(out=gains[:], in_=gain.rearrange("(g p t) -> p g t", p=P, t=PACK))

        put(3, list3, first[3])
        first.append(first_values(6))
        v2 = [gather_words(tab2[0], list2, "v2_0")]
        put(4, list3, first[4])
        first.append(first_values(7))
        gate2 = deal_gate(wg2_raw, "gate2_", "spread_then_plan1")
        v2.extend([gather_words(tab2[a], list2, "v2_%d" % a) for a in range(1, K2 // PASS)])
        put(5, list3, first[5])
        second = []
        for s in range(AHEAD):
            second.append(second_values(s))
            put(SLICES - AHEAD + s, list3, first[SLICES - AHEAD + s])

        w3_raw = [load_weight(w3, g, 0, "w3_%d" % g) for g in range(H // PASS)]
        plans = {(g, 0): load_plan(g, 0, keep, "spread_then_plan%d" % g) for g in range(H // PASS)}
        for g in range(H // PASS):
            plans[g, 1] = load_plan(g, 1, ring, "ring")

        for s in range(SLICES):
            if s + AHEAD < SLICES - 1:
                second.append(second_values(s + AHEAD))
            if s + AHEAD == SLICES - 1:
                second.append(second_values(SLICES - 1, "magnitude_then_w3", "back_then_w3", "angle_then_rows"))
            put(s, list4, second[s])
        w3q = [
            quantize_w3(w3_raw[0], "w3_0", "back_then_w3"),
            quantize_w3(w3_raw[1], "w3_1", "magnitude_then_w3"),
        ]

        out_view = out.rearrange("(m p) j -> p m j", p=P)
        tiles_n, passes = N // P, H // PASS
        for j0 in range(0, PJ, CHUNK):
            last = j0 + CHUNK == PJ
            xq = []
            for g in range(passes):
                if j0 == 0 and g == 0:
                    rows = keep.tile([P, PACK, CHUNK], BF16, name="rows", tag="angle_then_rows", align_bytes=64)
                else:
                    rows = work.tile([P, PACK, CHUNK], BF16, name="rows", tag="rows", bufs=X_DEPTH)
                xq.append(quantize_x(g, j0, rows, nc.vector.tensor_copy if last else nc.scalar.copy))
            staged = ring.tile([P, tiles_n, CHUNK], F32, name="staged", tag="ring", align_bytes=64)
            per_bank = 1 if last else 2
            banks = [bank([P, per_bank, CHUNK], "sums") for k in range(tiles_n // per_bank)]
            if last:
                steps = [(m, g) for g in range(passes) for m in range(tiles_n)]
            else:
                steps = [(m, g) for m in range(tiles_n) for g in range(passes)]
            for m, g in steps:
                k, place = divmod(m, per_bank)
                nc.tensor.matmul_mx(
                    out=banks[k][:, place, :],
                    lhsT=w3q[g][0][:, P * m : P * (m + 1)].bitcast(FP8X4),
                    lhsT_scale=w3q[g][1][:, P * m : P * (m + 1)],
                    rhs=xq[g][0][:].bitcast(FP8X4),
                    rhs_scale=xq[g][1][:],
                    start=(g == 0),
                    stop=(g == passes - 1),
                )
                if g == passes - 1 and place == per_bank - 1:
                    copy = nc.vector.tensor_copy if last and k % 2 == 1 else nc.scalar.copy
                    copy(out=staged[:, per_bank * k : per_bank * (k + 1), :], in_=banks[k][:])
                if last and g == passes - 1 and m % 2 == 1:
                    nc.sync.dma_start(out=out_view[:, m - 1 : m + 1, j0 : j0 + CHUNK], in_=staged[:, m - 1 : m + 1, :])
            if not last:
                nc.sync.dma_start(out=out_view[:, :, j0 : j0 + CHUNK], in_=staged[:])
